import numpy as np
import ml_dtypes


def mxq(x, axis, fmt="e4m3"):
    dtype, down = {"e4m3": (ml_dtypes.float8_e4m3fn, 7), "e5m2": (ml_dtypes.float8_e5m2, 14)}[fmt]
    v = np.moveaxis(np.asarray(x, np.float32).astype(ml_dtypes.bfloat16).astype(np.float64), axis, -1)
    blocks = v.reshape(v.shape[:-1] + (-1, 32))
    amax = np.abs(blocks).max(-1, keepdims=True)
    byte = np.maximum(np.where(amax > 0, np.frexp(amax)[1] - 1 + 127, 0) - down, 1)
    scale = np.exp2(byte - 127.0)
    codes = (blocks / scale).astype(np.float32).astype(dtype).astype(np.float64)
    return np.moveaxis((codes * scale).reshape(v.shape), -1, axis)


WIDE = False


def mx_kscale(k):
    if not WIDE:
        return np.ones(k)
    levels = np.array([10, -10, 5, -5, 0])
    if k % 512:
        return np.exp2(np.random.permutation(np.resize(levels, k // 32))).repeat(32)
    a = np.empty((k // 512, 16))
    for p in range(k // 512):
        a[p, :8] = np.random.permutation(np.resize(levels, 8))
        for g in range(8):
            far = levels[np.abs(levels - a[p, g]) >= 10]
            a[p, g + 8] = far[np.random.randint(len(far))]
    return np.exp2(a.ravel()).repeat(32)


def f64(x):
    return np.asarray(x).astype(np.float64)


def striped(idx):
    return np.tile(idx.reshape(-1, 16).T, (8, 1)).astype(np.uint16)


def unstriped(offs):
    return offs[:16].T.reshape(-1).astype(np.int64)


def striped8(idx):
    return np.concatenate([x.reshape(-1, 16).T for x in idx]).astype(np.uint16)


def runs(offs, k):
    lists = np.stack([offs[16 * r : 16 * r + 16].T.reshape(-1) for r in range(8)]).astype(np.int64)
    return lists[np.arange(k) % 512 // 64]


def pack_weight(w):
    k, n = w.shape
    w = f64(np.asarray(w, np.float32).astype(ml_dtypes.bfloat16)).reshape(k // 32, 32, n)
    amax = np.abs(w).max(1)
    byte = np.clip(np.where(amax > 0, np.frexp(amax)[1] - 1 + 127 - 7, 1), 1, 254)
    scaled = (w * np.exp2(127.0 - byte)[:, None, :]).reshape(k, n).astype(np.float32)
    words = np.ascontiguousarray(scaled.reshape(k // 512, 128, 4, n).transpose(0, 1, 3, 2)).astype(ml_dtypes.float8_e4m3fn).view(np.uint8)
    return words, np.ascontiguousarray(byte.astype(np.uint8).reshape(k // 512, 16, n))


def unpack_weight(words, scales):
    g, p, n, _ = words.shape
    vals = np.ascontiguousarray(words).view(ml_dtypes.float8_e4m3fn).astype(np.float64) * np.repeat(np.exp2(scales.astype(np.float64) - 127.0), 8, axis=1)[..., None]
    return vals.transpose(0, 1, 3, 2).reshape(g * 512, n)


K, T, S, N, G, H = 512, 2048, 512, 512, 2048, 512


def setup_inputs():
    n = np.random.standard_normal
    s = mx_kscale(K)[:, None]
    u = mx_kscale(H)
    packed_xT = pack_weight(n((K, T)) * s)
    packed_dT = pack_weight(n((K, G)) / s)
    return {
        "x_words": packed_xT[0],
        "x_scales": packed_xT[1],
        "d_words": packed_dT[0],
        "d_scales": packed_dT[1],
        "gn": (np.random.uniform(0.5, 1.5, (H, 1)) * u[:, None]).astype(np.float32),
        "w1": (n((H, N)) / np.sqrt(H) / u[:, None]).astype(np.float32),
        "offs": striped(np.random.permutation(T)[:S]),
        "kidx": striped8(np.random.randint(0, G, (8, H))),
        "n1": striped8(np.stack([np.random.permutation(S) for _ in range(8)])),
        "n2": striped8(np.stack([np.random.permutation(S) for _ in range(8)])),
    }


def reference(x_words, x_scales, d_words, d_scales, gn, w1, offs, kidx, n1, n2):
    d_kidx = unpack_weight(d_words, d_scales)[np.arange(K)[:, None], runs(kidx, K)]
    xq = unpack_weight(x_words, x_scales)[:, unstriped(offs)]
    s = 0.0625 * (d_kidx.T @ xq)
    z = f64(gn) * ((s[np.arange(H)[:, None], runs(n1, H)]) * (np.tanh(s - (s[np.arange(H)[:, None], runs(n2, H)]))))
    return mxq(f64(w1), 0, "e4m3").T @ mxq(z, 0, "e4m3")

@@ -1,0 +1,223 @@
+from contextlib import ExitStack
+
+import concourse.mybir as mybir
+
+K, T, S, N, G, H = 512, 2048, 512, 512, 2048, 512
+FLOPS = 2 * K * H * S + 2 * H * N * S
+
+F32 = mybir.dt.float32
+BF16 = mybir.dt.bfloat16
+I32 = mybir.dt.int32
+U32 = mybir.dt.uint32
+U16 = mybir.dt.uint16
+U8 = mybir.dt.uint8
+FP8X4 = mybir.dt.float8_e4m3fn_x4
+ACT = mybir.ActivationFunctionType
+ALU = mybir.AluOpType
+
+P = 128
+PACK = 4
+HALF = S // 2
+QUARTER = S // 4
+SCORE_SCALE = 0.0625
+
+
+def entries(offsets, first, count):
+    return offsets[:, first // 16 : (first + count) // 16]
+
+
+def tile_picked_scoretan_none_p_kernel(
+    tc, x_words, x_scales, d_words, d_scales, gn, w1, offs, kidx, n1, n2, out
+):
+    nc = tc.nc
+    with ExitStack() as ctx:
+        lists = ctx.enter_context(tc.tile_pool(name="lists", bufs=1))
+        sb = ctx.enter_context(tc.tile_pool(name="sb", bufs=1))
+        psum = ctx.enter_context(tc.psum_pool(name="psum", bufs=1))
+
+        d_scale_table = sb.tile([P, G], U8, name="d_scale_table")
+        x_scale_table = sb.tile([P, T], U8, name="x_scale_table")
+        nc.vector.memset(d_scale_table[:].bitcast(I32), 0)
+        nc.gpsimd.memset(x_scale_table[:].bitcast(I32), 0)
+        nc.scalar.dma_start(d_scale_table[0:P:8, :].bitcast(I32), d_scales[0].bitcast(I32))
+        nc.scalar.dma_start(x_scale_table[0:P:8, :].bitcast(I32), x_scales[0].bitcast(I32))
+
+        kidx_sb = lists.tile([P, H // 16], U16, name="kidx_sb")
+        offs_sb = lists.tile([P, S // 16], U16, name="offs_sb")
+        n2_sb = lists.tile([P, S // 16], U16, name="n2_sb")
+        n1_sb = lists.tile([P, S // 16], U16, name="n1_sb")
+        nc.sync.dma_start(kidx_sb[:], kidx)
+        nc.sync.dma_start(offs_sb[:], offs)
+
+        d_word_table = sb.tile([P, G], U32, name="d_word_table", tag="table_then_w1")
+        x_word_table = sb.tile([P, T], U32, name="x_word_table")
+        nc.sync.dma_start(d_word_table[:].bitcast(I32), d_words[0].rearrange("p n r -> p (n r)").bitcast(I32))
+        nc.sync.dma_start(n2_sb[:], n2)
+        nc.sync.dma_start(x_word_table[:].bitcast(I32), x_words[0].rearrange("p n r -> p (n r)").bitcast(I32))
+        nc.sync.dma_start(n1_sb[:], n1)
+        gn_sb = sb.tile([P, PACK], F32, name="gn_sb")
+        nc.scalar.dma_start(gn_sb[:], gn.rearrange("(p t) one -> p (t one)", t=PACK))
+
+        d_scale_picked = sb.tile([P, H], U8, name="d_scale_picked")
+        x_scale_picked = sb.tile([P, S], U8, name="x_scale_picked", tag="picked")
+        nc.vector.tensor_copy(d_scale_picked[:], d_scale_table[:].indirect(kidx_sb[:]))
+        nc.vector.tensor_copy(x_scale_picked[:], x_scale_table[:].indirect(offs_sb[:]))
+        scales = sb.tile([P, H + S], U8, name="scales", align_bytes=64)
+        nc.vector.tensor_copy(
+            scales[:, 0:H].rearrange("p (t m) -> p m t", t=PACK),
+            d_scale_picked[:].rearrange("p (m t) -> p m t", t=PACK),
+        )
+        nc.vector.tensor_copy(scales[:, H : H + S].bitcast(I32), x_scale_picked[:].bitcast(I32))
+        for row in range(1, 4):
+            nc.scalar.dma_start(scales[row:P:32, :].bitcast(I32), scales[8 * row : P : 32, :].bitcast(I32))
+
+        d_picked = sb.tile([P, H], U32, name="d_picked", tag="picked")
+        nc.vector.tensor_copy(d_picked[:], d_word_table[:].indirect(kidx_sb[:]))
+
+        gain = sb.tile([P, PACK], F32, name="gain")
+        safe = sb.tile([P, PACK], F32, name="safe")
+        undo = sb.tile([P, PACK], F32, name="undo")
+        nc.vector.scalar_tensor_tensor(safe[:], gn_sb[:], 0.0, gn_sb[:], ALU.is_equal, ALU.subtract)
+        nc.scalar.activation(gain[:], gn_sb[:], ACT.Copy, scale=SCORE_SCALE)
+        nc.vector.reciprocal(undo[:], safe[:])
+
+        keys = sb.tile([P, H], U32, name="keys", align_bytes=64)
+        nc.vector.tensor_copy(
+            keys[:].rearrange("p (t m) -> p m t", t=PACK),
+            d_picked[:].rearrange("p (m t) -> p m t", t=PACK),
+        )
+        queries = sb.tile([P, S], U32, name="queries", align_bytes=64)
+        for first in (0, HALF):
+            nc.vector.tensor_copy(
+                queries[:, first : first + HALF], x_word_table[:].indirect(entries(offs_sb, first, HALF))
+            )
+
+        w_raw = sb.tile([P, PACK, N], F32, name="w_raw", tag="table_then_w1")
+        nc.sync.dma_start(w_raw[:], w1.rearrange("(p t) m -> p t m", t=PACK))
+
+        def score(bank, t, first, count):
+            nc.tensor.matmul_mx(
+                out=bank,
+                lhsT=keys[:, t * P : (t + 1) * P].bitcast(FP8X4),
+                lhsT_scale=scales[:, t * P : (t + 1) * P],
+                rhs=queries[:, first : first + count].bitcast(FP8X4),
+                rhs_scale=scales[:, H + first : H + first + count],
+                start=True,
+                stop=True,
+            )
+
+        window = [sb.tile([P, S], F32, name="window%d" % t) for t in range(PACK)]
+        own = [[sb.tile([P, HALF], F32, name="own%d_%d" % (t, h)) for h in range(2)] for t in range(PACK)]
+        diff = [[sb.tile([P, HALF], F32, name="diff%d_%d" % (t, h)) for h in range(2)] for t in range(PACK)]
+        weight = [[sb.tile([P, HALF], F32, name="weight%d_%d" % (t, h)) for h in range(2)] for t in range(PACK)]
+
+        def scores_out(t):
+            if t == 0:
+                low = psum.tile([P, HALF], F32, name="score_low", tag="score_low")
+                high = psum.tile([P, HALF], F32, name="score_high", tag="score_high")
+                score(low[:], t, 0, HALF)
+                score(high[:], t, HALF, HALF)
+                nc.scalar.activation(window[t][:, 0:HALF], low[:], ACT.Copy, scale=gain[:, t : t + 1])
+                nc.scalar.activation(own[t][0][:], low[:], ACT.Copy, scale=gain[:, t : t + 1])
+                nc.vector.tensor_scalar(window[t][:, HALF:S], high[:], gain[:, t : t + 1], None, ALU.mult)
+            else:
+                bank = psum.tile([P, S], F32, name="score%d" % t)
+                score(bank[:], t, 0, S)
+                nc.scalar.activation(window[t][:], bank[:], ACT.Copy, scale=gain[:, t : t + 1])
+                nc.scalar.activation(own[t][0][:], bank[:, 0:HALF], ACT.Copy, scale=gain[:, t : t + 1])
+            nc.sync.dma_start(own[t][1][:], window[t][:, HALF:S])
+
+        def differ(t, h):
+            nc.vector.tensor_tensor(
+                diff[t][h][:], window[t][:].indirect(entries(n2_sb, h * HALF, HALF)), own[t][h][:], ALU.subtract
+            )
+            nc.scalar.activation(weight[t][h][:], diff[t][h][:], ACT.Tanh, scale=undo[:, t : t + 1])
+
+        chunks = ((0, HALF), (HALF, QUARTER), (HALF + QUARTER, QUARTER))
+        z = [sb.tile([P, PACK, count], F32, name="z%d" % c) for c, (first, count) in enumerate(chunks)]
+
+        def weigh(t, c):
+            first, count = chunks[c]
+            h, inside = divmod(first, HALF)
+            nc.vector.tensor_tensor(
+                z[c][:, t, :],
+                window[t][:].indirect(entries(n1_sb, first, count)),
+                weight[t][h][:, inside : inside + count],
+                ALU.mult,
+            )
+
+        def interleave(copy, packed, rows):
+            copy(packed.rearrange("p (c i t) -> p c t i", i=4, t=PACK), rows.rearrange("p t (c i) -> p c t i", i=4))
+
+        w_packed = sb.tile([P, N * PACK], BF16, name="w_packed", align_bytes=64)
+        w_codes = sb.tile([P, N], U32, name="w_codes", align_bytes=64)
+        w_scales = sb.tile([P, N], U8, name="w_scales", align_bytes=64)
+
+        def pack_w(a):
+            interleave(
+                nc.scalar.copy, w_packed[:, a * P * PACK : (a + 1) * P * PACK], w_raw[:, :, a * P : (a + 1) * P]
+            )
+
+        z_packed = [
+            sb.tile([P, count * PACK], BF16, name="z_packed%d" % c, align_bytes=64)
+            for c, (first, count) in enumerate(chunks)
+        ]
+        z_codes = [sb.tile([P, count], U32, name="z_codes%d" % c, align_bytes=64) for c, (first, count) in enumerate(chunks)]
+        z_scales = [sb.tile([P, count], U8, name="z_scales%d" % c, align_bytes=64) for c, (first, count) in enumerate(chunks)]
+        out_rows = out.rearrange("(a p) j -> p a j", p=P)
+
+        def quantize_z(c):
+            nc.vector.quantize_mx(out=z_codes[c][:].bitcast(FP8X4), scales=z_scales[c][:], in_=z_packed[c][:])
+
+        def project(c, tags, copies, queues):
+            first, count = chunks[c]
+            per = PACK // len(tags)
+            for b, tag in enumerate(tags):
+                bank = psum.tile([P, per, count], F32, name="out%d_%d" % (c, b), tag=tag)
+                for a in range(per):
+                    m = (b * per + a) * P
+                    nc.tensor.matmul_mx(
+                        out=bank[:, a, :],
+                        lhsT=w_codes[:, m : m + P].bitcast(FP8X4),
+                        lhsT_scale=w_scales[:, m : m + P],
+                        rhs=z_codes[c][:].bitcast(FP8X4),
+                        rhs_scale=z_scales[c][:],
+                        start=True,
+                        stop=True,
+                    )
+                staged = sb.tile([P, per, count], F32, name="staged%d_%d" % (c, b))
+                copies[b](staged[:], bank[:])
+                queues[b].dma_start(out_rows[:, b * per : (b + 1) * per, first : first + count], staged[:])
+
+        scores_out(0)
+        scores_out(1)
+        differ(0, 0)
+        differ(1, 0)
+        scores_out(2)
+        weigh(0, 0)
+        differ(2, 0)
+        scores_out(3)
+        weigh(1, 0)
+        differ(3, 0)
+        weigh(2, 0)
+        differ(0, 1)
+        weigh(3, 0)
+        for a in range(PACK):
+            pack_w(a)
+        differ(1, 1)
+        interleave(nc.scalar.copy, z_packed[0][:], z[0][:])
+        differ(2, 1)
+        differ(3, 1)
+        nc.vector.quantize_mx(out=w_codes[:].bitcast(FP8X4), scales=w_scales[:], in_=w_packed[:])
+        for t in range(PACK):
+            weigh(t, 1)
+        quantize_z(0)
+        interleave(nc.scalar.copy, z_packed[1][:], z[1][:])
+        project(0, ("out_a", "out_b"), (nc.scalar.copy, nc.scalar.copy), (nc.sync, nc.sync))
+        for t in range(PACK):
+            weigh(t, 2)
+        quantize_z(1)
+        interleave(nc.vector.tensor_copy, z_packed[2][:], z[2][:])
+        project(1, ("out_c",), (nc.scalar.copy,), (nc.sync,))
+        quantize_z(2)
+        project(2, ("score_low", "score_high"), (nc.scalar.copy, nc.vector.tensor_copy), (nc.scalar, nc.sync))

@@ -39,24 +39,27 @@ def tile_picked_scoretan_none_p_kernel(
         x_scale_table = sb.tile([P, T], U8, name="x_scale_table")
         nc.vector.memset(d_scale_table[:].bitcast(I32), 0)
         nc.gpsimd.memset(x_scale_table[:].bitcast(I32), 0)
-        nc.scalar.dma_start(d_scale_table[0:P:8, :].bitcast(I32), d_scales[0].bitcast(I32))
-        nc.scalar.dma_start(x_scale_table[0:P:8, :].bitcast(I32), x_scales[0].bitcast(I32))
 
         kidx_sb = lists.tile([P, H // 16], U16, name="kidx_sb")
         offs_sb = lists.tile([P, S // 16], U16, name="offs_sb")
         n2_sb = lists.tile([P, S // 16], U16, name="n2_sb")
         n1_sb = lists.tile([P, S // 16], U16, name="n1_sb")
+        d_word_table = sb.tile([P, G], U32, name="d_word_table", tag="table_then_w1")
+        x_word_table = sb.tile([P, T], U32, name="x_word_table", tag="table_then_w1b")
+        gn_sb = sb.tile([P, PACK], F32, name="gn_sb")
+        d_rows = d_words[0].rearrange("p n r -> p (n r)").bitcast(I32)
+        x_rows = x_words[0].rearrange("p n r -> p (n r)").bitcast(I32)
+        lead = 256
         nc.sync.dma_start(kidx_sb[:], kidx)
         nc.sync.dma_start(offs_sb[:], offs)
-
-        d_word_table = sb.tile([P, G], U32, name="d_word_table", tag="table_then_w1")
-        x_word_table = sb.tile([P, T], U32, name="x_word_table")
-        nc.sync.dma_start(d_word_table[:].bitcast(I32), d_words[0].rearrange("p n r -> p (n r)").bitcast(I32))
+        nc.sync.dma_start(gn_sb[:], gn.rearrange("(p t) one -> p (t one)", t=PACK))
+        nc.sync.dma_start(d_word_table[:, 0:lead].bitcast(I32), d_rows[:, 0:lead])
+        nc.sync.dma_start(d_scale_table[0:P:8, :].bitcast(I32), d_scales[0].bitcast(I32))
+        nc.sync.dma_start(x_scale_table[0:P:8, :].bitcast(I32), x_scales[0].bitcast(I32))
+        nc.sync.dma_start(d_word_table[:, lead:G].bitcast(I32), d_rows[:, lead:G])
+        nc.sync.dma_start(x_word_table[:].bitcast(I32), x_rows)
         nc.sync.dma_start(n2_sb[:], n2)
-        nc.sync.dma_start(x_word_table[:].bitcast(I32), x_words[0].rearrange("p n r -> p (n r)").bitcast(I32))
         nc.sync.dma_start(n1_sb[:], n1)
-        gn_sb = sb.tile([P, PACK], F32, name="gn_sb")
-        nc.scalar.dma_start(gn_sb[:], gn.rearrange("(p t) one -> p (t one)", t=PACK))
 
         d_scale_picked = sb.tile([P, H], U8, name="d_scale_picked")
         x_scale_picked = sb.tile([P, S], U8, name="x_scale_picked", tag="picked")
@@ -92,8 +95,11 @@ def tile_picked_scoretan_none_p_kernel(
                 queries[:, first : first + HALF], x_word_table[:].indirect(entries(offs_sb, first, HALF))
             )
 
-        w_raw = sb.tile([P, PACK, N], F32, name="w_raw", tag="table_then_w1")
-        nc.sync.dma_start(w_raw[:], w1.rearrange("(p t) m -> p t m", t=PACK))
+        w_rows = w1.rearrange("(p t) m -> p t m", t=PACK)
+        w_raw = []
+        for h, tag in enumerate(("table_then_w1", "table_then_w1b")):
+            w_raw.append(sb.tile([P, PACK, N // 2], F32, name="w_raw%d" % h, tag=tag))
+            nc.sync.dma_start(w_raw[h][:], w_rows[:, :, h * N // 2 : (h + 1) * N // 2])
 
         def score(bank, t, first, count):
             nc.tensor.matmul_mx(
@@ -120,21 +126,25 @@ def tile_picked_scoretan_none_p_kernel(
                 nc.scalar.activation(window[t][:, 0:HALF], low[:], ACT.Copy, scale=gain[:, t : t + 1])
                 nc.scalar.activation(own[t][0][:], low[:], ACT.Copy, scale=gain[:, t : t + 1])
                 nc.vector.tensor_scalar(window[t][:, HALF:S], high[:], gain[:, t : t + 1], None, ALU.mult)
+                nc.scalar.activation(own[t][1][:], high[:], ACT.Copy, scale=gain[:, t : t + 1])
             else:
                 bank = psum.tile([P, S], F32, name="score%d" % t)
                 score(bank[:], t, 0, S)
                 nc.scalar.activation(window[t][:], bank[:], ACT.Copy, scale=gain[:, t : t + 1])
                 nc.scalar.activation(own[t][0][:], bank[:, 0:HALF], ACT.Copy, scale=gain[:, t : t + 1])
-            nc.sync.dma_start(own[t][1][:], window[t][:, HALF:S])
+                nc.sync.dma_start(own[t][1][:], window[t][:, HALF:S])
 
         def differ(t, h):
             nc.vector.tensor_tensor(
                 diff[t][h][:], window[t][:].indirect(entries(n2_sb, h * HALF, HALF)), own[t][h][:], ALU.subtract
             )
+
+        def squash(t, h):
             nc.scalar.activation(weight[t][h][:], diff[t][h][:], ACT.Tanh, scale=undo[:, t : t + 1])
 
         chunks = ((0, HALF), (HALF, QUARTER), (HALF + QUARTER, QUARTER))
-        z = [sb.tile([P, PACK, count], F32, name="z%d" % c) for c, (first, count) in enumerate(chunks)]
+        z_tags = ("z0", "z1", "packed0")
+        packed_tags = ("packed0", "packed1", "packed1")
 
         def weigh(t, c):
             first, count = chunks[c]
@@ -149,19 +159,26 @@ def tile_picked_scoretan_none_p_kernel(
         def interleave(copy, packed, rows):
             copy(packed.rearrange("p (c i t) -> p c t i", i=4, t=PACK), rows.rearrange("p t (c i) -> p c t i", i=4))
 
-        w_packed = sb.tile([P, N * PACK], BF16, name="w_packed", align_bytes=64)
+        w_packed = [sb.tile([P, N // 2 * PACK], BF16, name="w_packed%d" % h, align_bytes=64) for h in range(2)]
         w_codes = sb.tile([P, N], U32, name="w_codes", align_bytes=64)
         w_scales = sb.tile([P, N], U8, name="w_scales", align_bytes=64)
 
-        def pack_w(a):
-            interleave(
-                nc.scalar.copy, w_packed[:, a * P * PACK : (a + 1) * P * PACK], w_raw[:, :, a * P : (a + 1) * P]
-            )
+        def pack_w(h):
+            interleave(nc.scalar.copy, w_packed[h][:], w_raw[h][:])
 
-        z_packed = [
-            sb.tile([P, count * PACK], BF16, name="z_packed%d" % c, align_bytes=64)
-            for c, (first, count) in enumerate(chunks)
-        ]
+        def quantize_w(h):
+            columns = slice(h * N // 2, (h + 1) * N // 2)
+            nc.vector.quantize_mx(out=w_codes[:, columns].bitcast(FP8X4), scales=w_scales[:, columns], in_=w_packed[h][:])
+
+        z, z_packed = {}, {}
+
+        def open_z(c):
+            z[c] = sb.tile([P, PACK, chunks[c][1]], F32, name="z%d" % c, tag=z_tags[c], align_bytes=64)
+
+        def pack_z(c, copy):
+            z_packed[c] = sb.tile([P, chunks[c][1] * PACK], BF16, name="z_packed%d" % c, tag=packed_tags[c], align_bytes=64)
+            interleave(copy, z_packed[c][:], z[c][:])
+
         z_codes = [sb.tile([P, count], U32, name="z_codes%d" % c, align_bytes=64) for c, (first, count) in enumerate(chunks)]
         z_scales = [sb.tile([P, count], U8, name="z_scales%d" % c, align_bytes=64) for c, (first, count) in enumerate(chunks)]
         out_rows = out.rearrange("(a p) j -> p a j", p=P)
@@ -190,34 +207,48 @@ def tile_picked_scoretan_none_p_kernel(
                 queues[b].dma_start(out_rows[:, b * per : (b + 1) * per, first : first + count], staged[:])
 
         scores_out(0)
-        scores_out(1)
         differ(0, 0)
+        differ(0, 1)
+        scores_out(1)
+        squash(0, 0)
         differ(1, 0)
-        scores_out(2)
+        open_z(0)
         weigh(0, 0)
+        scores_out(2)
+        squash(1, 0)
         differ(2, 0)
-        scores_out(3)
         weigh(1, 0)
+        scores_out(3)
+        squash(2, 0)
         differ(3, 0)
         weigh(2, 0)
-        differ(0, 1)
-        weigh(3, 0)
-        for a in range(PACK):
-            pack_w(a)
+        pack_w(0)
+        squash(3, 0)
         differ(1, 1)
-        interleave(nc.scalar.copy, z_packed[0][:], z[0][:])
+        weigh(3, 0)
         differ(2, 1)
+        quantize_w(0)
         differ(3, 1)
-        nc.vector.quantize_mx(out=w_codes[:].bitcast(FP8X4), scales=w_scales[:], in_=w_packed[:])
+        pack_w(1)
+        squash(0, 1)
+        squash(1, 1)
+        quantize_w(1)
+        pack_z(0, nc.scalar.copy)
+        squash(2, 1)
+        squash(3, 1)
+        open_z(1)
         for t in range(PACK):
             weigh(t, 1)
         quantize_z(0)
-        interleave(nc.scalar.copy, z_packed[1][:], z[1][:])
+        pack_z(1, nc.scalar.copy)
         project(0, ("out_a", "out_b"), (nc.scalar.copy, nc.scalar.copy), (nc.sync, nc.sync))
-        for t in range(PACK):
-            weigh(t, 2)
+        open_z(2)
+        weigh(0, 2)
+        weigh(1, 2)
         quantize_z(1)
-        interleave(nc.vector.tensor_copy, z_packed[2][:], z[2][:])
+        weigh(2, 2)
+        weigh(3, 2)
+        pack_z(2, nc.vector.tensor_copy)
         project(1, ("out_c",), (nc.scalar.copy,), (nc.sync,))
         quantize_z(2)
         project(2, ("score_low", "score_high"), (nc.scalar.copy, nc.vector.tensor_copy), (nc.scalar, nc.sync))

@@ -17,13 +17,24 @@ ALU = mybir.AluOpType
 
 P = 128
 PACK = 4
-HALF = S // 2
-QUARTER = S // 4
+BLOCK = 8
+QUADRANT = 32
 SCORE_SCALE = 0.0625
+HALF = S // 2
+CHUNKS = ((0, HALF), (HALF, S // 4), (HALF + S // 4, S // 4))
+LEAD = 256
 
 
 def entries(offsets, first, count):
     return offsets[:, first // 16 : (first + count) // 16]
+
+
+def interleave(copy, packed, rows):
+    copy(packed.rearrange("p (c i t) -> p c t i", i=4, t=PACK), rows.rearrange("p t (c i) -> p c t i", i=4))
+
+
+def deal(nc, dealt, picked):
+    nc.vector.tensor_copy(dealt.rearrange("p (t m) -> p m t", t=PACK), picked.rearrange("p (m t) -> p m t", t=PACK))
 
 
 def tile_picked_scoretan_none_p_kernel(
@@ -44,62 +55,52 @@ def tile_picked_scoretan_none_p_kernel(
         offs_sb = lists.tile([P, S // 16], U16, name="offs_sb")
         n2_sb = lists.tile([P, S // 16], U16, name="n2_sb")
         n1_sb = lists.tile([P, S // 16], U16, name="n1_sb")
-        d_word_table = sb.tile([P, G], U32, name="d_word_table", tag="table_then_w1")
-        x_word_table = sb.tile([P, T], U32, name="x_word_table", tag="table_then_w1b")
+        d_word_table = sb.tile([P, G], U32, name="d_word_table")
+        x_word_table = sb.tile([P, T], U32, name="x_word_table", tag="x_words_then_w1")
         gn_sb = sb.tile([P, PACK], F32, name="gn_sb")
         d_rows = d_words[0].rearrange("p n r -> p (n r)").bitcast(I32)
         x_rows = x_words[0].rearrange("p n r -> p (n r)").bitcast(I32)
-        lead = 256
         nc.sync.dma_start(kidx_sb[:], kidx)
         nc.sync.dma_start(offs_sb[:], offs)
         nc.sync.dma_start(gn_sb[:], gn.rearrange("(p t) one -> p (t one)", t=PACK))
-        nc.sync.dma_start(d_word_table[:, 0:lead].bitcast(I32), d_rows[:, 0:lead])
-        nc.sync.dma_start(d_scale_table[0:P:8, :].bitcast(I32), d_scales[0].bitcast(I32))
-        nc.sync.dma_start(x_scale_table[0:P:8, :].bitcast(I32), x_scales[0].bitcast(I32))
-        nc.sync.dma_start(d_word_table[:, lead:G].bitcast(I32), d_rows[:, lead:G])
+        nc.sync.dma_start(d_word_table[:, 0:LEAD].bitcast(I32), d_rows[:, 0:LEAD])
+        nc.sync.dma_start(d_scale_table[0:P:BLOCK, :].bitcast(I32), d_scales[0].bitcast(I32))
+        nc.sync.dma_start(x_scale_table[0:P:BLOCK, :].bitcast(I32), x_scales[0].bitcast(I32))
+        nc.sync.dma_start(d_word_table[:, LEAD:G].bitcast(I32), d_rows[:, LEAD:G])
         nc.sync.dma_start(x_word_table[:].bitcast(I32), x_rows)
         nc.sync.dma_start(n2_sb[:], n2)
         nc.sync.dma_start(n1_sb[:], n1)
 
         d_scale_picked = sb.tile([P, H], U8, name="d_scale_picked")
-        x_scale_picked = sb.tile([P, S], U8, name="x_scale_picked", tag="picked")
+        x_scale_picked = sb.tile([P, S], U8, name="x_scale_picked", tag="x_scales_then_d_words")
         nc.vector.tensor_copy(d_scale_picked[:], d_scale_table[:].indirect(kidx_sb[:]))
         nc.vector.tensor_copy(x_scale_picked[:], x_scale_table[:].indirect(offs_sb[:]))
         scales = sb.tile([P, H + S], U8, name="scales", align_bytes=64)
-        nc.vector.tensor_copy(
-            scales[:, 0:H].rearrange("p (t m) -> p m t", t=PACK),
-            d_scale_picked[:].rearrange("p (m t) -> p m t", t=PACK),
-        )
+        deal(nc, scales[:, 0:H], d_scale_picked[:])
         nc.vector.tensor_copy(scales[:, H : H + S].bitcast(I32), x_scale_picked[:].bitcast(I32))
-        for row in range(1, 4):
-            nc.scalar.dma_start(scales[row:P:32, :].bitcast(I32), scales[8 * row : P : 32, :].bitcast(I32))
+        for a in range(1, QUADRANT // BLOCK):
+            nc.scalar.dma_start(
+                scales[a:P:QUADRANT, :].bitcast(I32), scales[BLOCK * a : P : QUADRANT, :].bitcast(I32)
+            )
 
-        d_picked = sb.tile([P, H], U32, name="d_picked", tag="picked")
+        d_picked = sb.tile([P, H], U32, name="d_picked", tag="x_scales_then_d_words")
         nc.vector.tensor_copy(d_picked[:], d_word_table[:].indirect(kidx_sb[:]))
 
         gain = sb.tile([P, PACK], F32, name="gain")
-        safe = sb.tile([P, PACK], F32, name="safe")
+        divisor = sb.tile([P, PACK], F32, name="divisor")
         undo = sb.tile([P, PACK], F32, name="undo")
-        nc.vector.scalar_tensor_tensor(safe[:], gn_sb[:], 0.0, gn_sb[:], ALU.is_equal, ALU.subtract)
+        nc.vector.scalar_tensor_tensor(divisor[:], gn_sb[:], 0.0, gn_sb[:], ALU.is_equal, ALU.subtract)
         nc.scalar.activation(gain[:], gn_sb[:], ACT.Copy, scale=SCORE_SCALE)
-        nc.vector.reciprocal(undo[:], safe[:])
+        nc.vector.reciprocal(undo[:], divisor[:])
 
-        keys = sb.tile([P, H], U32, name="keys", align_bytes=64)
-        nc.vector.tensor_copy(
-            keys[:].rearrange("p (t m) -> p m t", t=PACK),
-            d_picked[:].rearrange("p (m t) -> p m t", t=PACK),
-        )
         queries = sb.tile([P, S], U32, name="queries", align_bytes=64)
-        for first in (0, HALF):
-            nc.vector.tensor_copy(
-                queries[:, first : first + HALF], x_word_table[:].indirect(entries(offs_sb, first, HALF))
-            )
+        nc.vector.tensor_copy(queries[:, 0:HALF], x_word_table[:].indirect(entries(offs_sb, 0, HALF)))
+        keys = sb.tile([P, H], U32, name="keys", align_bytes=64)
+        deal(nc, keys[:], d_picked[:])
+        nc.vector.tensor_copy(queries[:, HALF:S], x_word_table[:].indirect(entries(offs_sb, HALF, HALF)))
 
-        w_rows = w1.rearrange("(p t) m -> p t m", t=PACK)
-        w_raw = []
-        for h, tag in enumerate(("table_then_w1", "table_then_w1b")):
-            w_raw.append(sb.tile([P, PACK, N // 2], F32, name="w_raw%d" % h, tag=tag))
-            nc.sync.dma_start(w_raw[h][:], w_rows[:, :, h * N // 2 : (h + 1) * N // 2])
+        w_raw = sb.tile([P, PACK, N], F32, name="w_raw", tag="x_words_then_w1")
+        nc.sync.dma_start(w_raw[:], w1.rearrange("(p t) m -> p t m", t=PACK))
 
         def score(bank, t, first, count):
             nc.tensor.matmul_mx(
@@ -115,81 +116,76 @@ def tile_picked_scoretan_none_p_kernel(
         window = [sb.tile([P, S], F32, name="window%d" % t) for t in range(PACK)]
         own = [[sb.tile([P, HALF], F32, name="own%d_%d" % (t, h)) for h in range(2)] for t in range(PACK)]
         diff = [[sb.tile([P, HALF], F32, name="diff%d_%d" % (t, h)) for h in range(2)] for t in range(PACK)]
-        weight = [[sb.tile([P, HALF], F32, name="weight%d_%d" % (t, h)) for h in range(2)] for t in range(PACK)]
+        tanh = [[sb.tile([P, HALF], F32, name="tanh%d_%d" % (t, h)) for h in range(2)] for t in range(PACK)]
 
-        def scores_out(t):
-            if t == 0:
-                low = psum.tile([P, HALF], F32, name="score_low", tag="score_low")
-                high = psum.tile([P, HALF], F32, name="score_high", tag="score_high")
-                score(low[:], t, 0, HALF)
-                score(high[:], t, HALF, HALF)
-                nc.scalar.activation(window[t][:, 0:HALF], low[:], ACT.Copy, scale=gain[:, t : t + 1])
-                nc.scalar.activation(own[t][0][:], low[:], ACT.Copy, scale=gain[:, t : t + 1])
-                nc.vector.tensor_scalar(window[t][:, HALF:S], high[:], gain[:, t : t + 1], None, ALU.mult)
-                nc.scalar.activation(own[t][1][:], high[:], ACT.Copy, scale=gain[:, t : t + 1])
-            else:
-                bank = psum.tile([P, S], F32, name="score%d" % t)
-                score(bank[:], t, 0, S)
-                nc.scalar.activation(window[t][:], bank[:], ACT.Copy, scale=gain[:, t : t + 1])
-                nc.scalar.activation(own[t][0][:], bank[:, 0:HALF], ACT.Copy, scale=gain[:, t : t + 1])
-                nc.sync.dma_start(own[t][1][:], window[t][:, HALF:S])
+        def first_scores():
+            low = psum.tile([P, HALF], F32, name="score_low", tag="score_low")
+            high = psum.tile([P, HALF], F32, name="score_high", tag="score_high")
+            score(low[:], 0, 0, HALF)
+            score(high[:], 0, HALF, HALF)
+            nc.scalar.activation(window[0][:, 0:HALF], low[:], ACT.Copy, scale=gain[:, 0:1])
+            nc.scalar.activation(own[0][0][:], low[:], ACT.Copy, scale=gain[:, 0:1])
+            nc.vector.tensor_scalar(window[0][:, HALF:S], high[:], gain[:, 0:1], None, ALU.mult)
+            nc.scalar.activation(own[0][1][:], high[:], ACT.Copy, scale=gain[:, 0:1])
 
-        def differ(t, h):
+        def later_scores(t):
+            bank = psum.tile([P, S], F32, name="score%d" % t, tag="score%d" % t)
+            score(bank[:], t, 0, S)
+            nc.scalar.activation(window[t][:], bank[:], ACT.Copy, scale=gain[:, t : t + 1])
+            nc.scalar.activation(own[t][0][:], bank[:, 0:HALF], ACT.Copy, scale=gain[:, t : t + 1])
+            nc.sync.dma_start(own[t][1][:], window[t][:, HALF:S])
+
+        def subtract(t, h):
             nc.vector.tensor_tensor(
                 diff[t][h][:], window[t][:].indirect(entries(n2_sb, h * HALF, HALF)), own[t][h][:], ALU.subtract
             )
 
         def squash(t, h):
-            nc.scalar.activation(weight[t][h][:], diff[t][h][:], ACT.Tanh, scale=undo[:, t : t + 1])
+            nc.scalar.activation(tanh[t][h][:], diff[t][h][:], ACT.Tanh, scale=undo[:, t : t + 1])
 
-        chunks = ((0, HALF), (HALF, QUARTER), (HALF + QUARTER, QUARTER))
-        z_tags = ("z0", "z1", "packed0")
-        packed_tags = ("packed0", "packed1", "packed1")
-
-        def weigh(t, c):
-            first, count = chunks[c]
+        def multiply(t, c):
+            first, count = CHUNKS[c]
             h, inside = divmod(first, HALF)
             nc.vector.tensor_tensor(
                 z[c][:, t, :],
                 window[t][:].indirect(entries(n1_sb, first, count)),
-                weight[t][h][:, inside : inside + count],
+                tanh[t][h][:, inside : inside + count],
                 ALU.mult,
             )
 
-        def interleave(copy, packed, rows):
-            copy(packed.rearrange("p (c i t) -> p c t i", i=4, t=PACK), rows.rearrange("p t (c i) -> p c t i", i=4))
-
-        w_packed = [sb.tile([P, N // 2 * PACK], BF16, name="w_packed%d" % h, align_bytes=64) for h in range(2)]
+        w_packed = sb.tile([P, N * PACK], BF16, name="w_packed", align_bytes=64)
         w_codes = sb.tile([P, N], U32, name="w_codes", align_bytes=64)
         w_scales = sb.tile([P, N], U8, name="w_scales", align_bytes=64)
 
         def pack_w(h):
-            interleave(nc.scalar.copy, w_packed[h][:], w_raw[h][:])
+            first, last = h * N // 2, (h + 1) * N // 2
+            interleave(nc.scalar.copy, w_packed[:, first * PACK : last * PACK], w_raw[:, :, first:last])
 
-        def quantize_w(h):
-            columns = slice(h * N // 2, (h + 1) * N // 2)
-            nc.vector.quantize_mx(out=w_codes[:, columns].bitcast(FP8X4), scales=w_scales[:, columns], in_=w_packed[h][:])
-
+        z_tags = ("z0", "z1", "packed0")
+        packed_tags = ("packed0", "packed1", "packed1")
         z, z_packed = {}, {}
 
         def open_z(c):
-            z[c] = sb.tile([P, PACK, chunks[c][1]], F32, name="z%d" % c, tag=z_tags[c], align_bytes=64)
+            z[c] = sb.tile([P, PACK, CHUNKS[c][1]], F32, name="z%d" % c, tag=z_tags[c], align_bytes=64)
 
         def pack_z(c, copy):
-            z_packed[c] = sb.tile([P, chunks[c][1] * PACK], BF16, name="z_packed%d" % c, tag=packed_tags[c], align_bytes=64)
+            z_packed[c] = sb.tile(
+                [P, CHUNKS[c][1] * PACK], BF16, name="z_packed%d" % c, tag=packed_tags[c], align_bytes=64
+            )
             interleave(copy, z_packed[c][:], z[c][:])
 
-        z_codes = [sb.tile([P, count], U32, name="z_codes%d" % c, align_bytes=64) for c, (first, count) in enumerate(chunks)]
-        z_scales = [sb.tile([P, count], U8, name="z_scales%d" % c, align_bytes=64) for c, (first, count) in enumerate(chunks)]
+        widths = [count for first, count in CHUNKS]
+        z_codes = [sb.tile([P, count], U32, name="z_codes%d" % c, align_bytes=64) for c, count in enumerate(widths)]
+        z_scales = [sb.tile([P, count], U8, name="z_scales%d" % c, align_bytes=64) for c, count in enumerate(widths)]
         out_rows = out.rearrange("(a p) j -> p a j", p=P)
 
         def quantize_z(c):
             nc.vector.quantize_mx(out=z_codes[c][:].bitcast(FP8X4), scales=z_scales[c][:], in_=z_packed[c][:])
 
-        def project(c, tags, copies, queues):
-            first, count = chunks[c]
-            per = PACK // len(tags)
-            for b, tag in enumerate(tags):
+        def project(c, bank_tags, copies, queues):
+            first, count = CHUNKS[c]
+            per = N // P // len(bank_tags)
+            for b, tag in enumerate(bank_tags):
                 bank = psum.tile([P, per, count], F32, name="out%d_%d" % (c, b), tag=tag)
                 for a in range(per):
                     m = (b * per + a) * P
@@ -206,49 +202,48 @@ def tile_picked_scoretan_none_p_kernel(
                 copies[b](staged[:], bank[:])
                 queues[b].dma_start(out_rows[:, b * per : (b + 1) * per, first : first + count], staged[:])
 
-        scores_out(0)
-        differ(0, 0)
-        differ(0, 1)
-        scores_out(1)
-        squash(0, 0)
-        differ(1, 0)
+        first_scores()
+        subtract(0, 0)
+        subtract(0, 1)
         open_z(0)
-        weigh(0, 0)
-        scores_out(2)
-        squash(1, 0)
-        differ(2, 0)
-        weigh(1, 0)
-        scores_out(3)
-        squash(2, 0)
-        differ(3, 0)
-        weigh(2, 0)
+        for t in range(1, PACK):
+            later_scores(t)
+            squash(t - 1, 0)
+            subtract(t, 0)
+            multiply(t - 1, 0)
         pack_w(0)
-        squash(3, 0)
-        differ(1, 1)
-        weigh(3, 0)
-        differ(2, 1)
-        quantize_w(0)
-        differ(3, 1)
+        squash(PACK - 1, 0)
+        subtract(1, 1)
+        multiply(PACK - 1, 0)
+
+        subtract(2, 1)
+        subtract(3, 1)
         pack_w(1)
         squash(0, 1)
         squash(1, 1)
-        quantize_w(1)
-        pack_z(0, nc.scalar.copy)
+        nc.vector.quantize_mx(out=w_codes[:].bitcast(FP8X4), scales=w_scales[:], in_=w_packed[:])
         squash(2, 1)
         squash(3, 1)
+        pack_z(0, nc.scalar.copy)
+
         open_z(1)
         for t in range(PACK):
-            weigh(t, 1)
+            multiply(t, 1)
         quantize_z(0)
         pack_z(1, nc.scalar.copy)
         project(0, ("out_a", "out_b"), (nc.scalar.copy, nc.scalar.copy), (nc.sync, nc.sync))
         open_z(2)
-        weigh(0, 2)
-        weigh(1, 2)
+        multiply(0, 2)
+        multiply(1, 2)
         quantize_z(1)
-        weigh(2, 2)
-        weigh(3, 2)
+        multiply(2, 2)
+        multiply(3, 2)
         pack_z(2, nc.vector.tensor_copy)
         project(1, ("out_c",), (nc.scalar.copy,), (nc.sync,))
         quantize_z(2)
-        project(2, ("score_low", "score_high"), (nc.scalar.copy, nc.vector.tensor_copy), (nc.scalar, nc.sync))
+        project(
+            2,
+            ("score_low", "score_high", "score1", "score2"),
+            (nc.scalar.copy, nc.vector.tensor_copy) * 2,
+            (nc.scalar, nc.sync) * 2,
+        )

from contextlib import ExitStack

import concourse.mybir as mybir

K, T, S, N, G, H = 512, 2048, 512, 512, 2048, 512
FLOPS = 2 * K * H * S + 2 * H * N * S

F32 = mybir.dt.float32
BF16 = mybir.dt.bfloat16
I32 = mybir.dt.int32
U32 = mybir.dt.uint32
U16 = mybir.dt.uint16
U8 = mybir.dt.uint8
FP8X4 = mybir.dt.float8_e4m3fn_x4
ACT = mybir.ActivationFunctionType
ALU = mybir.AluOpType

P = 128
PACK = 4
BLOCK = 8
QUADRANT = 32
SCORE_SCALE = 0.0625
HALF = S // 2
CHUNKS = ((0, HALF), (HALF, S // 4), (HALF + S // 4, S // 4))
LEAD = 256


def entries(offsets, first, count):
    return offsets[:, first // 16 : (first + count) // 16]


def interleave(copy, packed, rows):
    copy(packed.rearrange("p (c i t) -> p c t i", i=4, t=PACK), rows.rearrange("p t (c i) -> p c t i", i=4))


def deal(nc, dealt, picked):
    nc.vector.tensor_copy(dealt.rearrange("p (t m) -> p m t", t=PACK), picked.rearrange("p (m t) -> p m t", t=PACK))


def tile_picked_scoretan_none_p_kernel(
    tc, x_words, x_scales, d_words, d_scales, gn, w1, offs, kidx, n1, n2, out
):
    nc = tc.nc
    with ExitStack() as ctx:
        lists = ctx.enter_context(tc.tile_pool(name="lists", bufs=1))
        sb = ctx.enter_context(tc.tile_pool(name="sb", bufs=1))
        psum = ctx.enter_context(tc.psum_pool(name="psum", bufs=1))

        d_scale_table = sb.tile([P, G], U8, name="d_scale_table")
        x_scale_table = sb.tile([P, T], U8, name="x_scale_table")
        nc.vector.memset(d_scale_table[:].bitcast(I32), 0)
        nc.gpsimd.memset(x_scale_table[:].bitcast(I32), 0)

        kidx_sb = lists.tile([P, H // 16], U16, name="kidx_sb")
        offs_sb = lists.tile([P, S // 16], U16, name="offs_sb")
        n2_sb = lists.tile([P, S // 16], U16, name="n2_sb")
        n1_sb = lists.tile([P, S // 16], U16, name="n1_sb")
        d_word_table = sb.tile([P, G], U32, name="d_word_table")
        x_word_table = sb.tile([P, T], U32, name="x_word_table", tag="x_words_then_w1")
        gn_sb = sb.tile([P, PACK], F32, name="gn_sb")
        d_rows = d_words[0].rearrange("p n r -> p (n r)").bitcast(I32)
        x_rows = x_words[0].rearrange("p n r -> p (n r)").bitcast(I32)
        nc.sync.dma_start(kidx_sb[:], kidx)
        nc.sync.dma_start(offs_sb[:], offs)
        nc.sync.dma_start(gn_sb[:], gn.rearrange("(p t) one -> p (t one)", t=PACK))
        nc.sync.dma_start(d_word_table[:, 0:LEAD].bitcast(I32), d_rows[:, 0:LEAD])
        nc.sync.dma_start(d_scale_table[0:P:BLOCK, :].bitcast(I32), d_scales[0].bitcast(I32))
        nc.sync.dma_start(x_scale_table[0:P:BLOCK, :].bitcast(I32), x_scales[0].bitcast(I32))
        nc.sync.dma_start(d_word_table[:, LEAD:G].bitcast(I32), d_rows[:, LEAD:G])
        nc.sync.dma_start(x_word_table[:].bitcast(I32), x_rows)
        nc.sync.dma_start(n2_sb[:], n2)
        nc.sync.dma_start(n1_sb[:], n1)

        d_scale_picked = sb.tile([P, H], U8, name="d_scale_picked")
        x_scale_picked = sb.tile([P, S], U8, name="x_scale_picked", tag="x_scales_then_d_words")
        nc.vector.tensor_copy(d_scale_picked[:], d_scale_table[:].indirect(kidx_sb[:]))
        nc.vector.tensor_copy(x_scale_picked[:], x_scale_table[:].indirect(offs_sb[:]))
        scales = sb.tile([P, H + S], U8, name="scales", align_bytes=64)
        deal(nc, scales[:, 0:H], d_scale_picked[:])
        nc.vector.tensor_copy(scales[:, H : H + S].bitcast(I32), x_scale_picked[:].bitcast(I32))
        for a in range(1, QUADRANT // BLOCK):
            nc.scalar.dma_start(
                scales[a:P:QUADRANT, :].bitcast(I32), scales[BLOCK * a : P : QUADRANT, :].bitcast(I32)
            )

        d_picked = sb.tile([P, H], U32, name="d_picked", tag="x_scales_then_d_words")
        nc.vector.tensor_copy(d_picked[:], d_word_table[:].indirect(kidx_sb[:]))

        gain = sb.tile([P, PACK], F32, name="gain")
        divisor = sb.tile([P, PACK], F32, name="divisor")
        undo = sb.tile([P, PACK], F32, name="undo")
        nc.vector.scalar_tensor_tensor(divisor[:], gn_sb[:], 0.0, gn_sb[:], ALU.is_equal, ALU.subtract)
        nc.scalar.activation(gain[:], gn_sb[:], ACT.Copy, scale=SCORE_SCALE)
        nc.vector.reciprocal(undo[:], divisor[:])

        queries = sb.tile([P, S], U32, name="queries", align_bytes=64)
        nc.vector.tensor_copy(queries[:, 0:HALF], x_word_table[:].indirect(entries(offs_sb, 0, HALF)))
        keys = sb.tile([P, H], U32, name="keys", align_bytes=64)
        deal(nc, keys[:], d_picked[:])
        nc.vector.tensor_copy(queries[:, HALF:S], x_word_table[:].indirect(entries(offs_sb, HALF, HALF)))

        w_raw = sb.tile([P, PACK, N], F32, name="w_raw", tag="x_words_then_w1")
        nc.sync.dma_start(w_raw[:], w1.rearrange("(p t) m -> p t m", t=PACK))

        def score(bank, t, first, count):
            nc.tensor.matmul_mx(
                out=bank,
                lhsT=keys[:, t * P : (t + 1) * P].bitcast(FP8X4),
                lhsT_scale=scales[:, t * P : (t + 1) * P],
                rhs=queries[:, first : first + count].bitcast(FP8X4),
                rhs_scale=scales[:, H + first : H + first + count],
                start=True,
                stop=True,
            )

        window = [sb.tile([P, S], F32, name="window%d" % t) for t in range(PACK)]
        own = [[sb.tile([P, HALF], F32, name="own%d_%d" % (t, h)) for h in range(2)] for t in range(PACK)]
        diff = [[sb.tile([P, HALF], F32, name="diff%d_%d" % (t, h)) for h in range(2)] for t in range(PACK)]
        tanh = [[sb.tile([P, HALF], F32, name="tanh%d_%d" % (t, h)) for h in range(2)] for t in range(PACK)]

        def first_scores():
            low = psum.tile([P, HALF], F32, name="score_low", tag="score_low")
            high = psum.tile([P, HALF], F32, name="score_high", tag="score_high")
            score(low[:], 0, 0, HALF)
            score(high[:], 0, HALF, HALF)
            nc.scalar.activation(window[0][:, 0:HALF], low[:], ACT.Copy, scale=gain[:, 0:1])
            nc.scalar.activation(own[0][0][:], low[:], ACT.Copy, scale=gain[:, 0:1])
            nc.vector.tensor_scalar(window[0][:, HALF:S], high[:], gain[:, 0:1], None, ALU.mult)
            nc.scalar.activation(own[0][1][:], high[:], ACT.Copy, scale=gain[:, 0:1])

        def later_scores(t):
            bank = psum.tile([P, S], F32, name="score%d" % t, tag="score%d" % t)
            score(bank[:], t, 0, S)
            nc.scalar.activation(window[t][:], bank[:], ACT.Copy, scale=gain[:, t : t + 1])
            nc.scalar.activation(own[t][0][:], bank[:, 0:HALF], ACT.Copy, scale=gain[:, t : t + 1])
            nc.sync.dma_start(own[t][1][:], window[t][:, HALF:S])

        def subtract(t, h):
            nc.vector.tensor_tensor(
                diff[t][h][:], window[t][:].indirect(entries(n2_sb, h * HALF, HALF)), own[t][h][:], ALU.subtract
            )

        def squash(t, h):
            nc.scalar.activation(tanh[t][h][:], diff[t][h][:], ACT.Tanh, scale=undo[:, t : t + 1])

        def multiply(t, c):
            first, count = CHUNKS[c]
            h, inside = divmod(first, HALF)
            nc.vector.tensor_tensor(
                z[c][:, t, :],
                window[t][:].indirect(entries(n1_sb, first, count)),
                tanh[t][h][:, inside : inside + count],
                ALU.mult,
            )

        w_packed = sb.tile([P, N * PACK], BF16, name="w_packed", align_bytes=64)
        w_codes = sb.tile([P, N], U32, name="w_codes", align_bytes=64)
        w_scales = sb.tile([P, N], U8, name="w_scales", align_bytes=64)

        def pack_w(h):
            first, last = h * N // 2, (h + 1) * N // 2
            interleave(nc.scalar.copy, w_packed[:, first * PACK : last * PACK], w_raw[:, :, first:last])

        z_tags = ("z0", "z1", "packed0")
        packed_tags = ("packed0", "packed1", "packed1")
        z, z_packed = {}, {}

        def open_z(c):
            z[c] = sb.tile([P, PACK, CHUNKS[c][1]], F32, name="z%d" % c, tag=z_tags[c], align_bytes=64)

        def pack_z(c, copy):
            z_packed[c] = sb.tile(
                [P, CHUNKS[c][1] * PACK], BF16, name="z_packed%d" % c, tag=packed_tags[c], align_bytes=64
            )
            interleave(copy, z_packed[c][:], z[c][:])

        widths = [count for first, count in CHUNKS]
        z_codes = [sb.tile([P, count], U32, name="z_codes%d" % c, align_bytes=64) for c, count in enumerate(widths)]
        z_scales = [sb.tile([P, count], U8, name="z_scales%d" % c, align_bytes=64) for c, count in enumerate(widths)]
        out_rows = out.rearrange("(a p) j -> p a j", p=P)

        def quantize_z(c):
            nc.vector.quantize_mx(out=z_codes[c][:].bitcast(FP8X4), scales=z_scales[c][:], in_=z_packed[c][:])

        def project(c, bank_tags, copies, queues):
            first, count = CHUNKS[c]
            per = N // P // len(bank_tags)
            for b, tag in enumerate(bank_tags):
                bank = psum.tile([P, per, count], F32, name="out%d_%d" % (c, b), tag=tag)
                for a in range(per):
                    m = (b * per + a) * P
                    nc.tensor.matmul_mx(
                        out=bank[:, a, :],
                        lhsT=w_codes[:, m : m + P].bitcast(FP8X4),
                        lhsT_scale=w_scales[:, m : m + P],
                        rhs=z_codes[c][:].bitcast(FP8X4),
                        rhs_scale=z_scales[c][:],
                        start=True,
                        stop=True,
                    )
                staged = sb.tile([P, per, count], F32, name="staged%d_%d" % (c, b))
                copies[b](staged[:], bank[:])
                queues[b].dma_start(out_rows[:, b * per : (b + 1) * per, first : first + count], staged[:])

        first_scores()
        subtract(0, 0)
        subtract(0, 1)
        open_z(0)
        for t in range(1, PACK):
            later_scores(t)
            squash(t - 1, 0)
            subtract(t, 0)
            multiply(t - 1, 0)
        pack_w(0)
        squash(PACK - 1, 0)
        subtract(1, 1)
        multiply(PACK - 1, 0)

        subtract(2, 1)
        subtract(3, 1)
        pack_w(1)
        squash(0, 1)
        squash(1, 1)
        nc.vector.quantize_mx(out=w_codes[:].bitcast(FP8X4), scales=w_scales[:], in_=w_packed[:])
        squash(2, 1)
        squash(3, 1)
        pack_z(0, nc.scalar.copy)

        open_z(1)
        for t in range(PACK):
            multiply(t, 1)
        quantize_z(0)
        pack_z(1, nc.scalar.copy)
        project(0, ("out_a", "out_b"), (nc.scalar.copy, nc.scalar.copy), (nc.sync, nc.sync))
        open_z(2)
        multiply(0, 2)
        multiply(1, 2)
        quantize_z(1)
        multiply(2, 2)
        multiply(3, 2)
        pack_z(2, nc.vector.tensor_copy)
        project(1, ("out_c",), (nc.scalar.copy,), (nc.sync,))
        quantize_z(2)
        project(
            2,
            ("score_low", "score_high", "score1", "score2"),
            (nc.scalar.copy, nc.vector.tensor_copy) * 2,
            (nc.scalar, nc.sync) * 2,
        )
